import numpy as np
import ml_dtypes


def mxq(x, axis, fmt="e4m3"):
    dtype, down = {"e4m3": (ml_dtypes.float8_e4m3fn, 7), "e5m2": (ml_dtypes.float8_e5m2, 14)}[fmt]
    v = np.moveaxis(np.asarray(x, np.float32).astype(ml_dtypes.bfloat16).astype(np.float64), axis, -1)
    blocks = v.reshape(v.shape[:-1] + (-1, 32))
    amax = np.abs(blocks).max(-1, keepdims=True)
    byte = np.maximum(np.where(amax > 0, np.frexp(amax)[1] - 1 + 127, 0) - down, 1)
    scale = np.exp2(byte - 127.0)
    codes = (blocks / scale).astype(np.float32).astype(dtype).astype(np.float64)
    return np.moveaxis((codes * scale).reshape(v.shape), -1, axis)


WIDE = False


def mx_kscale(k):
    if not WIDE:
        return np.ones(k)
    levels = np.array([30, -30])
    if k % 512:
        return np.exp2(np.random.permutation(np.resize(levels, k // 32))).repeat(32)
    a = np.empty((k // 512, 16))
    for p in range(k // 512):
        a[p, :8] = np.random.permutation(np.resize(levels, 8))
        for g in range(8):
            far = levels[np.abs(levels - a[p, g]) >= 10]
            a[p, g + 8] = far[np.random.randint(len(far))]
    return np.exp2(a.ravel()).repeat(32)


def f64(x):
    return np.asarray(x).astype(np.float64)


def striped(idx):
    return np.tile(np.asarray(idx).reshape(-1, 16).T, (8, 1)).astype(np.uint16)


def unstriped(offs):
    return offs[:16].T.reshape(-1).astype(np.int64)


E2M1 = np.array([0.0, 0.5, 1.0, 1.5, 2.0, 3.0, 4.0, 6.0, -0.0, -0.5, -1.0, -1.5, -2.0, -3.0, -4.0, -6.0])


def pack_weight(w, fmt):
    k, n = w.shape
    w = f64(np.asarray(w, np.float32).astype(ml_dtypes.bfloat16)).reshape(k // 32, 32, n)
    amax = np.abs(w).max(1)
    if fmt in ("e4m3", "e5m2"):
        byte = np.frexp(amax)[1] - 1 + 127 - (7 if fmt == "e4m3" else 14)
    else:
        mant, ex = np.frexp(amax / 6.0)
        byte = np.where(mant > 0.5, ex, ex - 1) + 127
    byte = np.clip(np.where(amax > 0, byte, 1), 1, 254)
    scaled = (w * np.exp2(127.0 - byte)[:, None, :]).reshape(k, n).astype(np.float32)
    by_word = np.ascontiguousarray(scaled.reshape(k // 512, 128, 4, n).transpose(0, 1, 3, 2))
    if fmt in ("e4m3", "e5m2"):
        words = by_word.astype(ml_dtypes.float8_e4m3fn if fmt == "e4m3" else ml_dtypes.float8_e5m2).view(np.uint8)
    else:
        c = by_word.astype(ml_dtypes.float4_e2m1fn).view(np.uint8) & 0xF
        words = (c[..., 0::2] | (c[..., 1::2] << 4)).reshape(k // 512, 128, 2 * n)
    return np.ascontiguousarray(words), np.ascontiguousarray(byte.astype(np.uint8).reshape(k // 512, 16, n))


def unpack_weight(words, scales, fmt):
    g, _, n = scales.shape
    words = np.ascontiguousarray(words).reshape(g, 128, n, -1)
    if fmt in ("e4m3", "e5m2"):
        vals = words.view(ml_dtypes.float8_e4m3fn if fmt == "e4m3" else ml_dtypes.float8_e5m2).astype(np.float64)
    else:
        nib = np.empty((g, 128, n, 4), np.uint8)
        nib[..., 0::2] = words & 0xF
        nib[..., 1::2] = words >> 4
        vals = E2M1[nib]
    vals = vals * np.repeat(np.exp2(scales.astype(np.float64) - 127.0), 8, axis=1)[..., None]
    return vals.transpose(0, 1, 3, 2).reshape(g * 512, n)


def e4m3fn_bytes(y):
    return np.clip(np.asarray(y, np.float64), -448.0, 448.0).astype(np.float32).astype(ml_dtypes.float8_e4m3fn).view(np.uint8)


def e4m3fn_values(b):
    return np.asarray(b, np.uint8).view(ml_dtypes.float8_e4m3fn).astype(np.float64)


K, V, O, U, F, T, Z = 512, 1024, 256, 256, 512, 1024, 1024


def setup_inputs():
    n = np.random.standard_normal
    idx = np.random.permutation(V)[:O]
    idx2 = np.random.permutation(V)[:U]
    idx3 = np.random.permutation(T)[:O]
    idx4 = np.random.permutation(Z)[:U]
    fk = mx_kscale(K)
    ff = mx_kscale(F)
    xtp = pack_weight(n((F, T)) / ff[:, None], "e2m1")
    xop = pack_weight(n((F, Z)) * 1 / np.sqrt(F) * ff[:, None], "e5m2")
    return {
        "ca": e4m3fn_bytes(60.0 * n((K, V))),
        "sa": (np.random.uniform(0.004, 0.012, (K, 1)) * fk[:, None]).astype(np.float32),
        "sb": (np.random.uniform(0.0002, 0.0006, (K, 1)) / fk[:, None]).astype(np.float32),
        "xt_words": xtp[0],
        "xt_scales": xtp[1],
        "xo_words": xop[0],
        "xo_scales": xop[1],
        "offs": striped(idx),
        "offs2": striped(idx2),
        "offs3": striped(idx3),
        "offs4": striped(idx4),
    }


def reference(ca, sa, sb, xt_words, xt_scales, xo_words, xo_scales, offs, offs2, offs3, offs4):
    idx = unstriped(offs)
    idx2 = unstriped(offs2)
    idx3 = unstriped(offs3)
    idx4 = unstriped(offs4)
    xtu = unpack_weight(xt_words, xt_scales, "e2m1")
    xou = unpack_weight(xo_words, xo_scales, "e5m2")
    z1 = e4m3fn_values(ca)[:, idx] * f64(sa)
    z2 = e4m3fn_values(ca)[:, idx2] * f64(sb)
    z1q = mxq(z1, 0, "e4m3")
    z2q = mxq(z2, 0, "e4m3")
    xtidx3g = xtu[:, idx3]
    xoidx4g = xou[:, idx4]
    p = z1q.T @ z2q + xtidx3g.T @ xoidx4g
    return p

@@ -1,0 +1,125 @@
+from contextlib import ExitStack
+
+import concourse.mybir as mybir
+
+K, V, O, U, F, T, Z = 512, 1024, 256, 256, 512, 1024, 1024
+FLOPS = 2 * O * U * (K + F)
+
+F32 = mybir.dt.float32
+BF16 = mybir.dt.bfloat16
+I32 = mybir.dt.int32
+U32 = mybir.dt.uint32
+U16 = mybir.dt.uint16
+U8 = mybir.dt.uint8
+FP8 = mybir.dt.float8_e4m3fn
+E4M3X4 = mybir.dt.float8_e4m3fn_x4
+E5M2X4 = mybir.dt.float8_e5m2_x4
+E2M1X4 = mybir.dt.float4_e2m1fn_x4
+COPY = mybir.ActivationFunctionType.Copy
+
+P = 128
+PACK = 4
+HALF = 128
+
+
+def tile_list_hybridscores_kernel(tc, ca, sa, sb, xt_words, xt_scales, xo_words, xo_scales, offs, offs2, offs3, offs4, out):
+    nc = tc.nc
+    with ExitStack() as ctx:
+        lists = ctx.enter_context(tc.tile_pool(name="lists", bufs=1))
+        sb_pool = ctx.enter_context(tc.tile_pool(name="work", bufs=1))
+        psum = ctx.enter_context(tc.psum_pool(name="psum", bufs=1))
+
+        def new(shape, dtype, name):
+            return sb_pool.tile(shape, dtype, name=name, align_bytes=64)
+
+        l_q = lists.tile([P, 16], U16, name="l_q")
+        l_c = lists.tile([P, 16], U16, name="l_c")
+        l_xt = lists.tile([P, 16], U16, name="l_xt")
+        l_xo = lists.tile([P, 16], U16, name="l_xo")
+        planes = [new([P, V], U8, "ca%d" % t) for t in range(PACK)]
+        step_q = new([P, PACK], F32, "step_q")
+        step_c = new([P, PACK], F32, "step_c")
+        xt_w = new([P, T], U16, "xt_w")
+        xo_w = new([P, Z], U32, "xo_w")
+        xt_s = new([P, T], U8, "xt_s")
+        xo_s = new([P, Z], U8, "xo_s")
+
+        warm_in = new([P, 1], F32, "warm_in")
+        warm_out = new([P, 1], F32, "warm_out")
+        nc.vector.memset(warm_in[:], 0.0)
+        nc.scalar.activation(warm_out[:], warm_in[:], COPY)
+        nc.vector.memset(xo_s[:].bitcast(I32), 0)
+        nc.vector.memset(xt_s[:].bitcast(I32), 0)
+
+        ca_planes = ca.rearrange("(p t) v -> t p v", t=PACK)
+        nc.sync.dma_start(planes[0][:], ca_planes[0])
+        nc.sync.dma_start(l_q[:], offs)
+        nc.sync.dma_start(step_q[:], sa.rearrange("(p t) o -> p (t o)", t=PACK))
+        for t in range(1, PACK):
+            nc.sync.dma_start(planes[t][:], ca_planes[t])
+        nc.sync.dma_start(l_c[:], offs2)
+        nc.sync.dma_start(step_c[:], sb.rearrange("(p t) o -> p (t o)", t=PACK))
+        for q in range(4):
+            nc.sync.dma_start(xo_s[32 * q : 32 * q + 4, :].bitcast(I32), xo_scales[0, 4 * q : 4 * q + 4, :].bitcast(I32))
+        nc.sync.dma_start(xo_w[:].bitcast(I32), xo_words[0].rearrange("p c r -> p (c r)").bitcast(I32))
+        nc.sync.dma_start(l_xo[:], offs4)
+        nc.sync.dma_start(xt_w[:].bitcast(I32), xt_words[0].bitcast(I32))
+        for q in range(4):
+            nc.sync.dma_start(xt_s[32 * q : 32 * q + 4, :].bitcast(I32), xt_scales[0, 4 * q : 4 * q + 4, :].bitcast(I32))
+        nc.sync.dma_start(l_xt[:], offs3)
+
+        def look_up(name, offsets, step):
+            picked = new([P, PACK, O], U8, name + "_bytes")
+            vals = sb_pool.tile([P, PACK, O], BF16, name=name + "_vals", tag="vals", align_bytes=64)
+            woven = new([P, O, PACK], BF16, name + "_woven")
+            for t in range(PACK):
+                nc.vector.tensor_copy(picked[:, t, :], planes[t][:].indirect(offsets[:]))
+                nc.scalar.activation(vals[:, t, :], picked[:, t, :].bitcast(FP8), COPY, scale=step[:, t : t + 1])
+            nc.scalar.copy(
+                woven[:].rearrange("p (c i) t -> p c t i", i=4),
+                vals[:].rearrange("p t (c i) -> p c t i", i=4),
+            )
+            return vals, woven
+
+        def quantise(name, woven, after):
+            codes = sb_pool.tile([P, O], U32, name=name + "_codes", tag=after, align_bytes=64)
+            scales = new([P, O], U8, name + "_scales")
+            nc.vector.quantize_mx(codes[:].bitcast(E4M3X4), scales[:], woven[:].rearrange("p c t -> p (c t)"))
+            return codes, scales
+
+        vals_q, woven_q = look_up("zq", l_q, step_q)
+        vals_c, woven_c = look_up("zc", l_c, step_c)
+
+        go_s = new([P, U], U8, "go_s")
+        go_w = new([P, U], U32, "go_w")
+        nc.vector.tensor_copy(go_w[:], xo_w[:].indirect(l_xo[:]))
+        nc.vector.tensor_copy(go_s[:], xo_s[:].indirect(l_xo[:]))
+        q_codes, q_scales = quantise("zq", woven_q, "xo_w")
+        c_codes, c_scales = quantise("zc", woven_c, "xo_s")
+        gt_w = sb_pool.tile([P, O], U16, name="gt_w", tag="zq_woven", align_bytes=64)
+        nc.vector.tensor_copy(gt_w[:], xt_w[:].indirect(l_xt[:]))
+        gt_s = sb_pool.tile([P, O], U8, name="gt_s", tag="zc_woven", align_bytes=64)
+        for h in range(2):
+            nc.vector.tensor_copy(gt_s[:, HALF * h : HALF * (h + 1)], xt_s[:].indirect(l_xt[:, 8 * h : 8 * h + 8]))
+
+        pieces = ((0, 0, 256), (1, 0, 128), (1, 128, 256))
+        banks = [psum.tile([P, b - a], F32, name="bank%d" % i) for i, (h, a, b) in enumerate(pieces)]
+        for bank, (h, a, b) in zip(banks, pieces):
+            rows = slice(HALF * h, HALF * (h + 1))
+            nc.tensor.matmul_mx(
+                bank[:], lhsT=q_codes[:, rows].bitcast(E4M3X4), lhsT_scale=q_scales[:, rows],
+                rhs=c_codes[:, a:b].bitcast(E4M3X4), rhs_scale=c_scales[:, a:b], start=True, stop=False,
+            )
+        for i, (bank, (h, a, b)) in enumerate(zip(banks, pieces)):
+            rows = slice(HALF * h, HALF * (h + 1))
+            nc.tensor.matmul_mx(
+                bank[:], lhsT=gt_w[:, rows].bitcast(E2M1X4), lhsT_scale=gt_s[:, rows],
+                rhs=go_w[:, a:b].bitcast(E5M2X4), rhs_scale=go_s[:, a:b], start=False, stop=True,
+            )
+            res = new([P, b - a], F32, "res%d" % i)
+            if i == 1:
+                nc.scalar.copy(res[:], bank[:])
+                nc.scalar.dma_start(out[rows, a:b], res[:])
+            else:
+                nc.vector.tensor_copy(res[:], bank[:])
+                nc.sync.dma_start(out[rows, a:b], res[:])

@@ -44,10 +44,6 @@ def tile_list_hybridscores_kernel(tc, ca, sa, sb, xt_words, xt_scales, xo_words,
         xt_s = new([P, T], U8, "xt_s")
         xo_s = new([P, Z], U8, "xo_s")
 
-        warm_in = new([P, 1], F32, "warm_in")
-        warm_out = new([P, 1], F32, "warm_out")
-        nc.vector.memset(warm_in[:], 0.0)
-        nc.scalar.activation(warm_out[:], warm_in[:], COPY)
         nc.vector.memset(xo_s[:].bitcast(I32), 0)
         nc.vector.memset(xt_s[:].bitcast(I32), 0)
 

@@ -27,6 +27,7 @@ def tile_list_hybridscores_kernel(tc, ca, sa, sb, xt_words, xt_scales, xo_words,
     with ExitStack() as ctx:
         lists = ctx.enter_context(tc.tile_pool(name="lists", bufs=1))
         sb_pool = ctx.enter_context(tc.tile_pool(name="work", bufs=1))
+        shared = ctx.enter_context(tc.tile_pool(name="shared", bufs=1))
         psum = ctx.enter_context(tc.psum_pool(name="psum", bufs=1))
 
         def new(shape, dtype, name):
@@ -40,7 +41,7 @@ def tile_list_hybridscores_kernel(tc, ca, sa, sb, xt_words, xt_scales, xo_words,
         step_q = new([P, PACK], F32, "step_q")
         step_c = new([P, PACK], F32, "step_c")
         xt_w = new([P, T], U16, "xt_w")
-        xo_w = new([P, Z], U32, "xo_w")
+        xo_w = shared.tile([P, Z], U32, name="xo_w", offset=0, align_bytes=64)
         xt_s = new([P, T], U8, "xt_s")
         xo_s = new([P, Z], U8, "xo_s")
 
@@ -49,65 +50,74 @@ def tile_list_hybridscores_kernel(tc, ca, sa, sb, xt_words, xt_scales, xo_words,
 
         ca_planes = ca.rearrange("(p t) v -> t p v", t=PACK)
         nc.sync.dma_start(planes[0][:], ca_planes[0])
-        nc.sync.dma_start(l_q[:], offs)
-        nc.sync.dma_start(step_q[:], sa.rearrange("(p t) o -> p (t o)", t=PACK))
-        for t in range(1, PACK):
-            nc.sync.dma_start(planes[t][:], ca_planes[t])
         nc.sync.dma_start(l_c[:], offs2)
         nc.sync.dma_start(step_c[:], sb.rearrange("(p t) o -> p (t o)", t=PACK))
+        for t in range(1, PACK):
+            nc.sync.dma_start(planes[t][:], ca_planes[t])
+        nc.sync.dma_start(l_q[:], offs)
+        nc.sync.dma_start(step_q[:], sa.rearrange("(p t) o -> p (t o)", t=PACK))
         for q in range(4):
             nc.sync.dma_start(xo_s[32 * q : 32 * q + 4, :].bitcast(I32), xo_scales[0, 4 * q : 4 * q + 4, :].bitcast(I32))
         nc.sync.dma_start(xo_w[:].bitcast(I32), xo_words[0].rearrange("p c r -> p (c r)").bitcast(I32))
-        nc.sync.dma_start(l_xo[:], offs4)
         nc.sync.dma_start(xt_w[:].bitcast(I32), xt_words[0].bitcast(I32))
         for q in range(4):
             nc.sync.dma_start(xt_s[32 * q : 32 * q + 4, :].bitcast(I32), xt_scales[0, 4 * q : 4 * q + 4, :].bitcast(I32))
         nc.sync.dma_start(l_xt[:], offs3)
+        nc.sync.dma_start(l_xo[:], offs4)
 
-        def look_up(name, offsets, step):
+        def look_up(name, offsets, step, parts):
             picked = new([P, PACK, O], U8, name + "_bytes")
-            vals = sb_pool.tile([P, PACK, O], BF16, name=name + "_vals", tag="vals", align_bytes=64)
-            woven = new([P, O, PACK], BF16, name + "_woven")
+            vals = sb_pool.tile([P, PACK, O], BF16, name=name + "_vals", align_bytes=64)
             for t in range(PACK):
                 nc.vector.tensor_copy(picked[:, t, :], planes[t][:].indirect(offsets[:]))
                 nc.scalar.activation(vals[:, t, :], picked[:, t, :].bitcast(FP8), COPY, scale=step[:, t : t + 1])
-            nc.scalar.copy(
-                woven[:].rearrange("p (c i) t -> p c t i", i=4),
-                vals[:].rearrange("p t (c i) -> p c t i", i=4),
-            )
-            return vals, woven
+            width = O // parts
+            woven = []
+            for j in range(parts):
+                w = new([P, width, PACK], BF16, name + "_woven%d" % j)
+                nc.scalar.copy(
+                    w[:].rearrange("p (c i) t -> p c t i", i=4),
+                    vals[:, :, j * width : (j + 1) * width].rearrange("p t (c i) -> p c t i", i=4),
+                )
+                woven.append(w)
+            return woven
 
         def quantise(name, woven, after):
-            codes = sb_pool.tile([P, O], U32, name=name + "_codes", tag=after, align_bytes=64)
-            scales = new([P, O], U8, name + "_scales")
+            width = woven.shape[1]
+            codes = shared.tile([P, width], U32, name=name + "_codes", offset=after, align_bytes=64)
+            scales = new([P, width], U8, name + "_scales")
             nc.vector.quantize_mx(codes[:].bitcast(E4M3X4), scales[:], woven[:].rearrange("p c t -> p (c t)"))
             return codes, scales
 
-        vals_q, woven_q = look_up("zq", l_q, step_q)
-        vals_c, woven_c = look_up("zc", l_c, step_c)
+        woven_c = look_up("zc", l_c, step_c, 1)
+        woven_q = look_up("zq", l_q, step_q, 2)
 
         go_s = new([P, U], U8, "go_s")
         go_w = new([P, U], U32, "go_w")
         nc.vector.tensor_copy(go_w[:], xo_w[:].indirect(l_xo[:]))
         nc.vector.tensor_copy(go_s[:], xo_s[:].indirect(l_xo[:]))
-        q_codes, q_scales = quantise("zq", woven_q, "xo_w")
-        c_codes, c_scales = quantise("zc", woven_c, "xo_s")
-        gt_w = sb_pool.tile([P, O], U16, name="gt_w", tag="zq_woven", align_bytes=64)
+        c_codes, c_scales = quantise("zc", woven_c[0], 0)
+        gt_w = shared.tile([P, O], U16, name="gt_w", offset=1024, align_bytes=64)
         nc.vector.tensor_copy(gt_w[:], xt_w[:].indirect(l_xt[:]))
-        gt_s = sb_pool.tile([P, O], U8, name="gt_s", tag="zc_woven", align_bytes=64)
+        gt_s = shared.tile([P, O], U8, name="gt_s", offset=1536, align_bytes=64)
+        q_ops = []
         for h in range(2):
+            q_ops.append(quantise("zq%d" % h, woven_q[h], 2048 + 512 * h))
             nc.vector.tensor_copy(gt_s[:, HALF * h : HALF * (h + 1)], xt_s[:].indirect(l_xt[:, 8 * h : 8 * h + 8]))
 
         pieces = ((0, 0, 256), (1, 0, 128), (1, 128, 256))
         banks = [psum.tile([P, b - a], F32, name="bank%d" % i) for i, (h, a, b) in enumerate(pieces)]
-        for bank, (h, a, b) in zip(banks, pieces):
-            rows = slice(HALF * h, HALF * (h + 1))
+        def z_pass(i):
+            h, a, b = pieces[i]
             nc.tensor.matmul_mx(
-                bank[:], lhsT=q_codes[:, rows].bitcast(E4M3X4), lhsT_scale=q_scales[:, rows],
+                banks[i][:], lhsT=q_ops[h][0][:].bitcast(E4M3X4), lhsT_scale=q_ops[h][1][:],
                 rhs=c_codes[:, a:b].bitcast(E4M3X4), rhs_scale=c_scales[:, a:b], start=True, stop=False,
             )
-        for i, (bank, (h, a, b)) in enumerate(zip(banks, pieces)):
+
+        def x_pass(i):
+            h, a, b = pieces[i]
             rows = slice(HALF * h, HALF * (h + 1))
+            bank = banks[i]
             nc.tensor.matmul_mx(
                 bank[:], lhsT=gt_w[:, rows].bitcast(E2M1X4), lhsT_scale=gt_s[:, rows],
                 rhs=go_w[:, a:b].bitcast(E5M2X4), rhs_scale=go_s[:, a:b], start=False, stop=True,
@@ -119,3 +129,10 @@ def tile_list_hybridscores_kernel(tc, ca, sa, sb, xt_words, xt_scales, xo_words,
             else:
                 nc.vector.tensor_copy(res[:], bank[:])
                 nc.sync.dma_start(out[rows, a:b], res[:])
+
+        z_pass(0)
+        x_pass(0)
+        z_pass(1)
+        z_pass(2)
+        x_pass(1)
+        x_pass(2)

@@ -45,6 +45,10 @@ def tile_list_hybridscores_kernel(tc, ca, sa, sb, xt_words, xt_scales, xo_words,
         xt_s = new([P, T], U8, "xt_s")
         xo_s = new([P, Z], U8, "xo_s")
 
+        warm_in = new([P, 1], F32, "warm_in")
+        warm_out = new([P, 1], F32, "warm_out")
+        nc.vector.memset(warm_in[:], 0.0)
+        nc.scalar.activation(warm_out[:], warm_in[:], COPY)
         nc.vector.memset(xo_s[:].bitcast(I32), 0)
         nc.vector.memset(xt_s[:].bitcast(I32), 0)
 

from contextlib import ExitStack

import concourse.mybir as mybir

K, V, O, U, F, T, Z = 512, 1024, 256, 256, 512, 1024, 1024
FLOPS = 2 * O * U * (K + F)

F32 = mybir.dt.float32
BF16 = mybir.dt.bfloat16
I32 = mybir.dt.int32
U32 = mybir.dt.uint32
U16 = mybir.dt.uint16
U8 = mybir.dt.uint8
FP8 = mybir.dt.float8_e4m3fn
E4M3X4 = mybir.dt.float8_e4m3fn_x4
E5M2X4 = mybir.dt.float8_e5m2_x4
E2M1X4 = mybir.dt.float4_e2m1fn_x4
COPY = mybir.ActivationFunctionType.Copy

P = 128
PACK = 4
HALF = 128


def tile_list_hybridscores_kernel(tc, ca, sa, sb, xt_words, xt_scales, xo_words, xo_scales, offs, offs2, offs3, offs4, out):
    nc = tc.nc
    with ExitStack() as ctx:
        lists = ctx.enter_context(tc.tile_pool(name="lists", bufs=1))
        sb_pool = ctx.enter_context(tc.tile_pool(name="work", bufs=1))
        shared = ctx.enter_context(tc.tile_pool(name="shared", bufs=1))
        psum = ctx.enter_context(tc.psum_pool(name="psum", bufs=1))

        def new(shape, dtype, name):
            return sb_pool.tile(shape, dtype, name=name, align_bytes=64)

        l_q = lists.tile([P, 16], U16, name="l_q")
        l_c = lists.tile([P, 16], U16, name="l_c")
        l_xt = lists.tile([P, 16], U16, name="l_xt")
        l_xo = lists.tile([P, 16], U16, name="l_xo")
        planes = [new([P, V], U8, "ca%d" % t) for t in range(PACK)]
        step_q = new([P, PACK], F32, "step_q")
        step_c = new([P, PACK], F32, "step_c")
        xt_w = new([P, T], U16, "xt_w")
        xo_w = shared.tile([P, Z], U32, name="xo_w", offset=0, align_bytes=64)
        xt_s = new([P, T], U8, "xt_s")
        xo_s = new([P, Z], U8, "xo_s")

        warm_in = new([P, 1], F32, "warm_in")
        warm_out = new([P, 1], F32, "warm_out")
        nc.vector.memset(warm_in[:], 0.0)
        nc.scalar.activation(warm_out[:], warm_in[:], COPY)
        nc.vector.memset(xo_s[:].bitcast(I32), 0)
        nc.vector.memset(xt_s[:].bitcast(I32), 0)

        ca_planes = ca.rearrange("(p t) v -> t p v", t=PACK)
        nc.sync.dma_start(planes[0][:], ca_planes[0])
        nc.sync.dma_start(l_c[:], offs2)
        nc.sync.dma_start(step_c[:], sb.rearrange("(p t) o -> p (t o)", t=PACK))
        for t in range(1, PACK):
            nc.sync.dma_start(planes[t][:], ca_planes[t])
        nc.sync.dma_start(l_q[:], offs)
        nc.sync.dma_start(step_q[:], sa.rearrange("(p t) o -> p (t o)", t=PACK))
        for q in range(4):
            nc.sync.dma_start(xo_s[32 * q : 32 * q + 4, :].bitcast(I32), xo_scales[0, 4 * q : 4 * q + 4, :].bitcast(I32))
        nc.sync.dma_start(xo_w[:].bitcast(I32), xo_words[0].rearrange("p c r -> p (c r)").bitcast(I32))
        nc.sync.dma_start(xt_w[:].bitcast(I32), xt_words[0].bitcast(I32))
        for q in range(4):
            nc.sync.dma_start(xt_s[32 * q : 32 * q + 4, :].bitcast(I32), xt_scales[0, 4 * q : 4 * q + 4, :].bitcast(I32))
        nc.sync.dma_start(l_xt[:], offs3)
        nc.sync.dma_start(l_xo[:], offs4)

        def look_up(name, offsets, step, parts):
            picked = new([P, PACK, O], U8, name + "_bytes")
            vals = sb_pool.tile([P, PACK, O], BF16, name=name + "_vals", align_bytes=64)
            for t in range(PACK):
                nc.vector.tensor_copy(picked[:, t, :], planes[t][:].indirect(offsets[:]))
                nc.scalar.activation(vals[:, t, :], picked[:, t, :].bitcast(FP8), COPY, scale=step[:, t : t + 1])
            width = O // parts
            woven = []
            for j in range(parts):
                w = new([P, width, PACK], BF16, name + "_woven%d" % j)
                nc.scalar.copy(
                    w[:].rearrange("p (c i) t -> p c t i", i=4),
                    vals[:, :, j * width : (j + 1) * width].rearrange("p t (c i) -> p c t i", i=4),
                )
                woven.append(w)
            return woven

        def quantise(name, woven, after):
            width = woven.shape[1]
            codes = shared.tile([P, width], U32, name=name + "_codes", offset=after, align_bytes=64)
            scales = new([P, width], U8, name + "_scales")
            nc.vector.quantize_mx(codes[:].bitcast(E4M3X4), scales[:], woven[:].rearrange("p c t -> p (c t)"))
            return codes, scales

        woven_c = look_up("zc", l_c, step_c, 1)
        woven_q = look_up("zq", l_q, step_q, 2)

        go_s = new([P, U], U8, "go_s")
        go_w = new([P, U], U32, "go_w")
        nc.vector.tensor_copy(go_w[:], xo_w[:].indirect(l_xo[:]))
        nc.vector.tensor_copy(go_s[:], xo_s[:].indirect(l_xo[:]))
        c_codes, c_scales = quantise("zc", woven_c[0], 0)
        gt_w = shared.tile([P, O], U16, name="gt_w", offset=1024, align_bytes=64)
        nc.vector.tensor_copy(gt_w[:], xt_w[:].indirect(l_xt[:]))
        gt_s = shared.tile([P, O], U8, name="gt_s", offset=1536, align_bytes=64)
        q_ops = []
        for h in range(2):
            q_ops.append(quantise("zq%d" % h, woven_q[h], 2048 + 512 * h))
            nc.vector.tensor_copy(gt_s[:, HALF * h : HALF * (h + 1)], xt_s[:].indirect(l_xt[:, 8 * h : 8 * h + 8]))

        pieces = ((0, 0, 256), (1, 0, 128), (1, 128, 256))
        banks = [psum.tile([P, b - a], F32, name="bank%d" % i) for i, (h, a, b) in enumerate(pieces)]
        def z_pass(i):
            h, a, b = pieces[i]
            nc.tensor.matmul_mx(
                banks[i][:], lhsT=q_ops[h][0][:].bitcast(E4M3X4), lhsT_scale=q_ops[h][1][:],
                rhs=c_codes[:, a:b].bitcast(E4M3X4), rhs_scale=c_scales[:, a:b], start=True, stop=False,
            )

        def x_pass(i):
            h, a, b = pieces[i]
            rows = slice(HALF * h, HALF * (h + 1))
            bank = banks[i]
            nc.tensor.matmul_mx(
                bank[:], lhsT=gt_w[:, rows].bitcast(E2M1X4), lhsT_scale=gt_s[:, rows],
                rhs=go_w[:, a:b].bitcast(E5M2X4), rhs_scale=go_s[:, a:b], start=False, stop=True,
            )
            res = new([P, b - a], F32, "res%d" % i)
            if i == 1:
                nc.scalar.copy(res[:], bank[:])
                nc.scalar.dma_start(out[rows, a:b], res[:])
            else:
                nc.vector.tensor_copy(res[:], bank[:])
                nc.sync.dma_start(out[rows, a:b], res[:])

        z_pass(0)
        x_pass(0)
        z_pass(1)
        z_pass(2)
        x_pass(1)
        x_pass(2)
